import numpy as np
import ml_dtypes


def mxq(x, axis, fmt="e4m3"):
    dtype, down = {"e4m3": (ml_dtypes.float8_e4m3fn, 7), "e5m2": (ml_dtypes.float8_e5m2, 14)}[fmt]
    v = np.moveaxis(np.asarray(x, np.float32).astype(ml_dtypes.bfloat16).astype(np.float64), axis, -1)
    blocks = v.reshape(v.shape[:-1] + (-1, 32))
    amax = np.abs(blocks).max(-1, keepdims=True)
    byte = np.maximum(np.where(amax > 0, np.frexp(amax)[1] - 1 + 127, 0) - down, 1)
    scale = np.exp2(byte - 127.0)
    codes = (blocks / scale).astype(np.float32).astype(dtype).astype(np.float64)
    return np.moveaxis((codes * scale).reshape(v.shape), -1, axis)


WIDE = False


def mx_kscale(k):
    if not WIDE:
        return np.ones(k)
    levels = np.array([10, -10, 5, -5, 0])
    if k % 512:
        return np.exp2(np.random.permutation(np.resize(levels, k // 32))).repeat(32)
    a = np.empty((k // 512, 16))
    for p in range(k // 512):
        a[p, :8] = np.random.permutation(np.resize(levels, 8))
        for g in range(8):
            far = levels[np.abs(levels - a[p, g]) >= 10]
            a[p, g + 8] = far[np.random.randint(len(far))]
    return np.exp2(a.ravel()).repeat(32)


def f64(x):
    return np.asarray(x).astype(np.float64)


def striped(idx):
    return np.tile(idx.reshape(-1, 16).T, (8, 1)).astype(np.uint16)


def unstriped(offs):
    return offs[:16].T.reshape(-1).astype(np.int64)


def pack_weight(w):
    k, n = w.shape
    w = f64(np.asarray(w, np.float32).astype(ml_dtypes.bfloat16)).reshape(k // 32, 32, n)
    amax = np.abs(w).max(1)
    byte = np.clip(np.where(amax > 0, np.frexp(amax)[1] - 1 + 127 - 7, 1), 1, 254)
    scaled = (w * np.exp2(127.0 - byte)[:, None, :]).reshape(k, n).astype(np.float32)
    words = np.ascontiguousarray(scaled.reshape(k // 512, 128, 4, n).transpose(0, 1, 3, 2)).astype(ml_dtypes.float8_e4m3fn).view(np.uint8)
    return words, np.ascontiguousarray(byte.astype(np.uint8).reshape(k // 512, 16, n))


def unpack_weight(words, scales):
    g, p, n, _ = words.shape
    vals = np.ascontiguousarray(words).view(ml_dtypes.float8_e4m3fn).astype(np.float64) * np.repeat(np.exp2(scales.astype(np.float64) - 127.0), 8, axis=1)[..., None]
    return vals.transpose(0, 1, 3, 2).reshape(g * 512, n)


def sigmoid(v):
    return 1.0 / (1.0 + np.exp(-np.maximum(v, -700.0)))


K, T, S, D, N = 512, 2048, 512, 4, 128


def setup_inputs():
    n = np.random.standard_normal
    s = mx_kscale(K)[:, None]
    packed_xT = pack_weight(n((K, T)) * s)
    return {
        "x_words": packed_xT[0],
        "x_scales": packed_xT[1],
        "w1": (n((K, N)) / np.sqrt(K) / s).astype(np.float32),
        "w2": (n((K, N)) / np.sqrt(K) / s).astype(np.float32),
        "offs": striped(np.random.permutation(T)[:S]),
    }


def reference(x_words, x_scales, w1, w2, offs):
    xq = unpack_weight(x_words, x_scales)[:, unstriped(offs)]
    ys = mxq(f64(w1), 0, "e4m3").T @ xq
    ls = np.log(sigmoid(ys) + 0.02)
    yu = mxq(f64(w2), 0, "e4m3").T @ xq
    iou = 0.9 * sigmoid(yu) + 0.05
    al = np.exp(0.5 * ls + 3.0 * np.log(iou))
    mi = iou.reshape(len(iou), -1, D).max(axis=2)
    mt = al.reshape(len(al), -1, D).max(axis=2) + 0.01
    nt = al * np.repeat(mi / mt, D, axis=1)
    ql = ((sigmoid(ys) - nt) ** 2) * (-1.0 * (nt * ls + (-1.0 * nt + 1.0) * (np.log(-1.0 * (0.98 * sigmoid(ys)) + 1.0))))
    return ql.reshape(len(ql), -1, D).sum(axis=2)

@@ -1,0 +1,146 @@
+from contextlib import ExitStack
+
+import concourse.mybir as mybir
+
+K, T, S, D, N = 512, 2048, 512, 4, 128
+P = 128
+PACK = 4
+HALVES = 2
+COLS = S // HALVES
+GROUPS = COLS // D
+LIST_COLS = COLS // 16
+
+F32 = mybir.dt.float32
+BF16 = mybir.dt.bfloat16
+I32 = mybir.dt.int32
+U32 = mybir.dt.uint32
+U16 = mybir.dt.uint16
+U8 = mybir.dt.uint8
+FP8X4 = mybir.dt.float8_e4m3fn_x4
+ALU = mybir.AluOpType
+ACT = mybir.ActivationFunctionType
+AXIS_X = mybir.AxisListType.X
+
+FLOPS = 2 * 2 * K * N * S
+
+
+def grouped(ap):
+    return ap.rearrange("p (v d) -> p v d", d=D)
+
+
+def tile_picked_ytal_loss_p_kernel(tc, x_words, x_scales, w1, w2, offs, out):
+    nc = tc.nc
+    halves = range(HALVES)
+    with ExitStack() as ctx:
+        sb = ctx.enter_context(tc.tile_pool(name="sb", bufs=1))
+        ps = ctx.enter_context(tc.psum_pool(name="ps", bufs=1))
+
+        def half_tiles(name, width, dtype=F32):
+            return [sb.tile([P, width], dtype, name=f"{name}{h}", align_bytes=64) for h in halves]
+
+        offsets = sb.tile([P, S // 16], U16, name="offsets")
+        scale_table = sb.tile([P, T], U8, name="scale_table", align_bytes=64)
+        word_table = sb.tile([P, T], I32, name="word_table", align_bytes=64)
+        nc.vector.memset(scale_table[:].bitcast(I32), 0)
+        nc.sync.dma_start(offsets[:], offs)
+        raw = {}
+        for name, w in (("u", w2), ("s", w1)):
+            raw[name] = sb.tile([P, PACK, N], F32, name=f"raw_{name}")
+            nc.sync.dma_start(raw[name][:], w.rearrange("(p j) m -> p j m", j=PACK))
+        for q in range(4):
+            nc.sync.dma_start(scale_table[32 * q : 32 * q + 4, :].bitcast(I32), x_scales[0, 4 * q : 4 * q + 4, :].bitcast(I32))
+        nc.sync.dma_start(word_table[:], x_words[0].rearrange("p c r -> p (c r)").bitcast(I32))
+
+        w_codes, w_scales = {}, {}
+        rounded = {}
+        for name in ("u", "s"):
+            rounded[name] = sb.tile([P, N, PACK], BF16, name=f"rounded_{name}", align_bytes=64)
+            w_codes[name] = sb.tile([P, N], U32, name=f"w_codes_{name}", align_bytes=64)
+            w_scales[name] = sb.tile([P, N], U8, name=f"w_scales_{name}", align_bytes=64)
+        nc.vector.tensor_copy(rounded["u"][:], raw["u"][:].rearrange("p j m -> p m j"))
+        nc.scalar.copy(rounded["s"][:], raw["s"][:].rearrange("p j m -> p m j"))
+        x_scale = sb.tile([P, S], U8, name="x_scale", align_bytes=64)
+        nc.vector.tensor_copy(x_scale[:], scale_table[:].indirect(offsets[:]))
+        for name in ("u", "s"):
+            nc.vector.quantize_mx(out=w_codes[name][:].bitcast(FP8X4), scales=w_scales[name][:],
+                                  in_=rounded[name][:].rearrange("p m j -> p (m j)"))
+
+        x_codes = half_tiles("x_codes", COLS, U32)
+        th = {name: half_tiles(f"th_{name}", COLS) for name in ("u", "s")}
+        for h in halves:
+            nc.vector.tensor_copy(x_codes[h][:], word_table[:].bitcast(U32).indirect(offsets[:, h * LIST_COLS : (h + 1) * LIST_COLS]))
+            for name in ("u", "s"):
+                y = ps.tile([P, COLS], F32, name=f"y_{name}{h}")
+                nc.tensor.matmul_mx(out=y[:], lhsT=w_codes[name][:].bitcast(FP8X4), lhsT_scale=w_scales[name][:],
+                                    rhs=x_codes[h][:].bitcast(FP8X4), rhs_scale=x_scale[:, h * COLS : (h + 1) * COLS],
+                                    start=True, stop=True)
+                nc.scalar.activation(th[name][h][:], y[:], ACT.Tanh, scale=0.5)
+
+        iou = half_tiles("iou", COLS)
+        iou2 = half_tiles("iou2", COLS)
+        iou3 = half_tiles("iou3", COLS)
+        iou6 = half_tiles("iou6", COLS)
+        z = half_tiles("z", COLS)
+        logs = sb.tile([P, 2 * HALVES, COLS], F32, name="logs")
+        zmax = [logs[:, 2 * h : 2 * h + 2, 0 : GROUPS // 2] for h in halves]
+        mi = half_tiles("mi", GROUPS)
+        for h in halves:
+            nc.vector.tensor_scalar(iou[h][:], th["u"][h][:], 0.45, 0.5, ALU.mult, ALU.add)
+        for h in halves:
+            nc.vector.tensor_tensor(iou2[h][:], iou[h][:], iou[h][:], ALU.mult)
+        for h in halves:
+            nc.vector.tensor_tensor(iou3[h][:], iou2[h][:], iou[h][:], ALU.mult)
+        for h in halves:
+            nc.vector.tensor_tensor(iou6[h][:], iou3[h][:], iou3[h][:], ALU.mult)
+        for h in halves:
+            nc.vector.scalar_tensor_tensor(z[h][:], th["s"][h][:], 1.04, iou6[h][:], ALU.add, ALU.mult)
+        for h in halves:
+            nc.vector.tensor_reduce(zmax[h], z[h][:].rearrange("p (a v d) -> p a v d", a=2, d=D), AXIS_X, ALU.max)
+        for h in halves:
+            nc.vector.tensor_reduce(mi[h][:], grouped(iou[h][:]), AXIS_X, ALU.max)
+
+        al = half_tiles("al", COLS)
+        almax = sb.tile([P, HALVES * GROUPS], F32, name="almax")
+        for h in halves:
+            nc.scalar.activation(al[h][:], z[h][:], ACT.Sqrt, scale=0.5)
+        nc.scalar.activation(almax[:].rearrange("p (a v) -> p a v", a=2 * HALVES), logs[:, :, 0 : GROUPS // 2], ACT.Sqrt, scale=0.5)
+        ls = [logs[:, 2 * h, :] for h in halves]
+        lb = [logs[:, 2 * h + 1, :] for h in halves]
+        for h in halves:
+            nc.scalar.activation(ls[h], th["s"][h][:], ACT.Ln, scale=0.5, bias=0.52)
+            nc.scalar.activation(lb[h], th["s"][h][:], ACT.Ln, scale=-0.49, bias=0.51)
+
+        mt = half_tiles("mt", GROUPS)
+        inv = half_tiles("inv", GROUPS)
+        ratio = half_tiles("ratio", GROUPS)
+        nt = half_tiles("nt", COLS)
+        gap = half_tiles("gap", COLS)
+        gap2 = half_tiles("gap2", COLS)
+        pos = half_tiles("pos", COLS)
+        neg = half_tiles("neg", COLS)
+        ce = half_tiles("ce", COLS)
+        ql = half_tiles("ql", COLS)
+        result = sb.tile([P, HALVES * GROUPS], F32, name="result")
+        for h in halves:
+            nc.vector.tensor_scalar(mt[h][:], almax[:, h * GROUPS : (h + 1) * GROUPS], 0.01, None, ALU.add)
+        for h in halves:
+            nc.vector.reciprocal(inv[h][:], mt[h][:])
+        for h in halves:
+            nc.vector.tensor_tensor(ratio[h][:], inv[h][:], mi[h][:], ALU.mult)
+        for h in halves:
+            nc.vector.tensor_tensor(grouped(nt[h][:]), grouped(al[h][:]), ratio[h][:].unsqueeze(2).to_broadcast([P, GROUPS, D]), ALU.mult)
+        for h in halves:
+            nc.vector.scalar_tensor_tensor(gap[h][:], th["s"][h][:], -0.5, nt[h][:], ALU.mult, ALU.add)
+        for h in halves:
+            nc.scalar.activation(gap2[h][:], gap[h][:], ACT.Square, bias=-0.5)
+        for h in halves:
+            nc.vector.tensor_tensor(pos[h][:], nt[h][:], ls[h], ALU.mult)
+        for h in halves:
+            nc.vector.scalar_tensor_tensor(neg[h][:], nt[h][:], -1.0, lb[h], ALU.add, ALU.mult)
+        for h in halves:
+            nc.vector.tensor_tensor(ce[h][:], neg[h][:], pos[h][:], ALU.subtract)
+        for h in halves:
+            nc.vector.tensor_tensor(ql[h][:], ce[h][:], gap2[h][:], ALU.mult)
+        for h in halves:
+            nc.vector.tensor_reduce(result[:, h * GROUPS : (h + 1) * GROUPS], grouped(ql[h][:]), AXIS_X, ALU.add)
+        nc.sync.dma_start(out, result[:])

@@ -1,3 +1,4 @@
+import math
 from contextlib import ExitStack
 
 import concourse.mybir as mybir
@@ -44,9 +45,9 @@ def tile_picked_ytal_loss_p_kernel(tc, x_words, x_scales, w1, w2, offs, out):
         nc.vector.memset(scale_table[:].bitcast(I32), 0)
         nc.sync.dma_start(offsets[:], offs)
         raw = {}
-        for name, w in (("u", w2), ("s", w1)):
+        for name, w, queue in (("u", w2, nc.sync), ("s", w1, nc.scalar)):
             raw[name] = sb.tile([P, PACK, N], F32, name=f"raw_{name}")
-            nc.sync.dma_start(raw[name][:], w.rearrange("(p j) m -> p j m", j=PACK))
+            queue.dma_start(raw[name][:], w.rearrange("(p j) m -> p j m", j=PACK))
         for q in range(4):
             nc.sync.dma_start(scale_table[32 * q : 32 * q + 4, :].bitcast(I32), x_scales[0, 4 * q : 4 * q + 4, :].bitcast(I32))
         nc.sync.dma_start(word_table[:], x_words[0].rearrange("p c r -> p (c r)").bitcast(I32))
@@ -66,7 +67,9 @@ def tile_picked_ytal_loss_p_kernel(tc, x_words, x_scales, w1, w2, offs, out):
                                   in_=rounded[name][:].rearrange("p m j -> p (m j)"))
 
         x_codes = half_tiles("x_codes", COLS, U32)
-        th = {name: half_tiles(f"th_{name}", COLS) for name in ("u", "s")}
+        th = {name: half_tiles(f"th_{name}", COLS) for name in ("u", "s", "odds")}
+        ys = []
+        iou2 = half_tiles("iou2", COLS)
         for h in halves:
             nc.vector.tensor_copy(x_codes[h][:], word_table[:].bitcast(U32).indirect(offsets[:, h * LIST_COLS : (h + 1) * LIST_COLS]))
             for name in ("u", "s"):
@@ -75,39 +78,43 @@ def tile_picked_ytal_loss_p_kernel(tc, x_words, x_scales, w1, w2, offs, out):
                                     rhs=x_codes[h][:].bitcast(FP8X4), rhs_scale=x_scale[:, h * COLS : (h + 1) * COLS],
                                     start=True, stop=True)
                 nc.scalar.activation(th[name][h][:], y[:], ACT.Tanh, scale=0.5)
+                if name == "u" and h == 1:
+                    nc.scalar.activation(iou2[h][:], th["u"][h][:], ACT.Square, scale=0.45, bias=0.5)
+            ys.append(y)
+        for h in halves:
+            nc.scalar.activation(th["odds"][h][:], ys[h][:], ACT.Tanh, scale=0.5, bias=-0.5 * math.log(50.0))
 
-        iou = half_tiles("iou", COLS)
-        iou2 = half_tiles("iou2", COLS)
-        iou3 = half_tiles("iou3", COLS)
+        iou = sb.tile([P, COLS], F32, name="iou")
+        iou4 = half_tiles("iou4", COLS)
         iou6 = half_tiles("iou6", COLS)
         z = half_tiles("z", COLS)
         logs = sb.tile([P, 2 * HALVES, COLS], F32, name="logs")
         zmax = [logs[:, 2 * h : 2 * h + 2, 0 : GROUPS // 2] for h in halves]
         mi = half_tiles("mi", GROUPS)
+        nc.vector.tensor_scalar(iou[:], th["u"][0][:], 0.45, 0.5, ALU.mult, ALU.add)
+        nc.vector.tensor_reduce(mi[0][:], grouped(th["u"][0][:]), AXIS_X, ALU.max)
+        nc.vector.tensor_tensor(iou2[0][:], iou[:], iou[:], ALU.mult)
+        nc.vector.tensor_reduce(mi[1][:], grouped(th["u"][1][:]), AXIS_X, ALU.max)
         for h in halves:
-            nc.vector.tensor_scalar(iou[h][:], th["u"][h][:], 0.45, 0.5, ALU.mult, ALU.add)
+            nc.vector.tensor_tensor(iou4[h][:], iou2[h][:], iou2[h][:], ALU.mult)
         for h in halves:
-            nc.vector.tensor_tensor(iou2[h][:], iou[h][:], iou[h][:], ALU.mult)
-        for h in halves:
-            nc.vector.tensor_tensor(iou3[h][:], iou2[h][:], iou[h][:], ALU.mult)
-        for h in halves:
-            nc.vector.tensor_tensor(iou6[h][:], iou3[h][:], iou3[h][:], ALU.mult)
+            nc.vector.tensor_tensor(iou6[h][:], iou4[h][:], iou2[h][:], ALU.mult)
         for h in halves:
             nc.vector.scalar_tensor_tensor(z[h][:], th["s"][h][:], 1.04, iou6[h][:], ALU.add, ALU.mult)
         for h in halves:
             nc.vector.tensor_reduce(zmax[h], z[h][:].rearrange("p (a v d) -> p a v d", a=2, d=D), AXIS_X, ALU.max)
-        for h in halves:
-            nc.vector.tensor_reduce(mi[h][:], grouped(iou[h][:]), AXIS_X, ALU.max)
 
-        al = half_tiles("al", COLS)
-        almax = sb.tile([P, HALVES * GROUPS], F32, name="almax")
+        al = z
+        almax = half_tiles("almax", GROUPS)
         for h in halves:
-            nc.scalar.activation(al[h][:], z[h][:], ACT.Sqrt, scale=0.5)
-        nc.scalar.activation(almax[:].rearrange("p (a v) -> p a v", a=2 * HALVES), logs[:, :, 0 : GROUPS // 2], ACT.Sqrt, scale=0.5)
+            nc.scalar.activation(almax[h][:].rearrange("p (a v) -> p a v", a=2), zmax[h], ACT.Sqrt, scale=0.5)
+        for h in halves:
+            nc.scalar.activation(al[h][:], z[h][:], ACT.Sqrt, scale=0.5 * 0.45 * 0.45)
         ls = [logs[:, 2 * h, :] for h in halves]
         lb = [logs[:, 2 * h + 1, :] for h in halves]
         for h in halves:
-            nc.scalar.activation(ls[h], th["s"][h][:], ACT.Ln, scale=0.5, bias=0.52)
+            nc.scalar.activation(ls[h], th["odds"][h][:], ACT.Ln, scale=25.49, bias=25.51)
+        for h in halves:
             nc.scalar.activation(lb[h], th["s"][h][:], ACT.Ln, scale=-0.49, bias=0.51)
 
         mt = half_tiles("mt", GROUPS)
@@ -117,16 +124,15 @@ def tile_picked_ytal_loss_p_kernel(tc, x_words, x_scales, w1, w2, offs, out):
         gap = half_tiles("gap", COLS)
         gap2 = half_tiles("gap2", COLS)
         pos = half_tiles("pos", COLS)
-        neg = half_tiles("neg", COLS)
         ce = half_tiles("ce", COLS)
         ql = half_tiles("ql", COLS)
         result = sb.tile([P, HALVES * GROUPS], F32, name="result")
         for h in halves:
-            nc.vector.tensor_scalar(mt[h][:], almax[:, h * GROUPS : (h + 1) * GROUPS], 0.01, None, ALU.add)
+            nc.vector.tensor_scalar(mt[h][:], almax[h][:], 0.01, None, ALU.add)
         for h in halves:
             nc.vector.reciprocal(inv[h][:], mt[h][:])
         for h in halves:
-            nc.vector.tensor_tensor(ratio[h][:], inv[h][:], mi[h][:], ALU.mult)
+            nc.vector.scalar_tensor_tensor(ratio[h][:], mi[h][:], 0.5 / 0.45, inv[h][:], ALU.add, ALU.mult)
         for h in halves:
             nc.vector.tensor_tensor(grouped(nt[h][:]), grouped(al[h][:]), ratio[h][:].unsqueeze(2).to_broadcast([P, GROUPS, D]), ALU.mult)
         for h in halves:
@@ -136,11 +142,9 @@ def tile_picked_ytal_loss_p_kernel(tc, x_words, x_scales, w1, w2, offs, out):
         for h in halves:
             nc.vector.tensor_tensor(pos[h][:], nt[h][:], ls[h], ALU.mult)
         for h in halves:
-            nc.vector.scalar_tensor_tensor(neg[h][:], nt[h][:], -1.0, lb[h], ALU.add, ALU.mult)
+            nc.vector.tensor_tensor(ce[h][:], pos[h][:], lb[h], ALU.add)
         for h in halves:
-            nc.vector.tensor_tensor(ce[h][:], neg[h][:], pos[h][:], ALU.subtract)
-        for h in halves:
-            nc.vector.tensor_tensor(ql[h][:], ce[h][:], gap2[h][:], ALU.mult)
+            nc.vector.scalar_tensor_tensor(ql[h][:], ce[h][:], -1.0, gap2[h][:], ALU.mult, ALU.mult)
         for h in halves:
             nc.vector.tensor_reduce(result[:, h * GROUPS : (h + 1) * GROUPS], grouped(ql[h][:]), AXIS_X, ALU.add)
         nc.sync.dma_start(out, result[:])

import math
from contextlib import ExitStack

import concourse.mybir as mybir

K, T, S, D, N = 512, 2048, 512, 4, 128
P = 128
PACK = 4
HALVES = 2
COLS = S // HALVES
GROUPS = COLS // D
LIST_COLS = COLS // 16

F32 = mybir.dt.float32
BF16 = mybir.dt.bfloat16
I32 = mybir.dt.int32
U32 = mybir.dt.uint32
U16 = mybir.dt.uint16
U8 = mybir.dt.uint8
FP8X4 = mybir.dt.float8_e4m3fn_x4
ALU = mybir.AluOpType
ACT = mybir.ActivationFunctionType
AXIS_X = mybir.AxisListType.X

FLOPS = 2 * 2 * K * N * S


def grouped(ap):
    return ap.rearrange("p (v d) -> p v d", d=D)


def tile_picked_ytal_loss_p_kernel(tc, x_words, x_scales, w1, w2, offs, out):
    nc = tc.nc
    halves = range(HALVES)
    with ExitStack() as ctx:
        sb = ctx.enter_context(tc.tile_pool(name="sb", bufs=1))
        ps = ctx.enter_context(tc.psum_pool(name="ps", bufs=1))

        def half_tiles(name, width, dtype=F32):
            return [sb.tile([P, width], dtype, name=f"{name}{h}", align_bytes=64) for h in halves]

        offsets = sb.tile([P, S // 16], U16, name="offsets")
        scale_table = sb.tile([P, T], U8, name="scale_table", align_bytes=64)
        word_table = sb.tile([P, T], I32, name="word_table", align_bytes=64)
        nc.vector.memset(scale_table[:].bitcast(I32), 0)
        nc.sync.dma_start(offsets[:], offs)
        raw = {}
        for name, w, queue in (("u", w2, nc.sync), ("s", w1, nc.scalar)):
            raw[name] = sb.tile([P, PACK, N], F32, name=f"raw_{name}")
            queue.dma_start(raw[name][:], w.rearrange("(p j) m -> p j m", j=PACK))
        for q in range(4):
            nc.sync.dma_start(scale_table[32 * q : 32 * q + 4, :].bitcast(I32), x_scales[0, 4 * q : 4 * q + 4, :].bitcast(I32))
        nc.sync.dma_start(word_table[:], x_words[0].rearrange("p c r -> p (c r)").bitcast(I32))

        w_codes, w_scales = {}, {}
        rounded = {}
        for name in ("u", "s"):
            rounded[name] = sb.tile([P, N, PACK], BF16, name=f"rounded_{name}", align_bytes=64)
            w_codes[name] = sb.tile([P, N], U32, name=f"w_codes_{name}", align_bytes=64)
            w_scales[name] = sb.tile([P, N], U8, name=f"w_scales_{name}", align_bytes=64)
        nc.vector.tensor_copy(rounded["u"][:], raw["u"][:].rearrange("p j m -> p m j"))
        nc.scalar.copy(rounded["s"][:], raw["s"][:].rearrange("p j m -> p m j"))
        x_scale = sb.tile([P, S], U8, name="x_scale", align_bytes=64)
        nc.vector.tensor_copy(x_scale[:], scale_table[:].indirect(offsets[:]))
        for name in ("u", "s"):
            nc.vector.quantize_mx(out=w_codes[name][:].bitcast(FP8X4), scales=w_scales[name][:],
                                  in_=rounded[name][:].rearrange("p m j -> p (m j)"))

        x_codes = half_tiles("x_codes", COLS, U32)
        th = {name: half_tiles(f"th_{name}", COLS) for name in ("u", "s", "odds")}
        ys = []
        iou2 = half_tiles("iou2", COLS)
        for h in halves:
            nc.vector.tensor_copy(x_codes[h][:], word_table[:].bitcast(U32).indirect(offsets[:, h * LIST_COLS : (h + 1) * LIST_COLS]))
            for name in ("u", "s"):
                y = ps.tile([P, COLS], F32, name=f"y_{name}{h}")
                nc.tensor.matmul_mx(out=y[:], lhsT=w_codes[name][:].bitcast(FP8X4), lhsT_scale=w_scales[name][:],
                                    rhs=x_codes[h][:].bitcast(FP8X4), rhs_scale=x_scale[:, h * COLS : (h + 1) * COLS],
                                    start=True, stop=True)
                nc.scalar.activation(th[name][h][:], y[:], ACT.Tanh, scale=0.5)
                if name == "u" and h == 1:
                    nc.scalar.activation(iou2[h][:], th["u"][h][:], ACT.Square, scale=0.45, bias=0.5)
            ys.append(y)
        for h in halves:
            nc.scalar.activation(th["odds"][h][:], ys[h][:], ACT.Tanh, scale=0.5, bias=-0.5 * math.log(50.0))

        iou = sb.tile([P, COLS], F32, name="iou")
        iou4 = half_tiles("iou4", COLS)
        iou6 = half_tiles("iou6", COLS)
        z = half_tiles("z", COLS)
        logs = sb.tile([P, 2 * HALVES, COLS], F32, name="logs")
        zmax = [logs[:, 2 * h : 2 * h + 2, 0 : GROUPS // 2] for h in halves]
        mi = half_tiles("mi", GROUPS)
        nc.vector.tensor_scalar(iou[:], th["u"][0][:], 0.45, 0.5, ALU.mult, ALU.add)
        nc.vector.tensor_reduce(mi[0][:], grouped(th["u"][0][:]), AXIS_X, ALU.max)
        nc.vector.tensor_tensor(iou2[0][:], iou[:], iou[:], ALU.mult)
        nc.vector.tensor_reduce(mi[1][:], grouped(th["u"][1][:]), AXIS_X, ALU.max)
        for h in halves:
            nc.vector.tensor_tensor(iou4[h][:], iou2[h][:], iou2[h][:], ALU.mult)
        for h in halves:
            nc.vector.tensor_tensor(iou6[h][:], iou4[h][:], iou2[h][:], ALU.mult)
        for h in halves:
            nc.vector.scalar_tensor_tensor(z[h][:], th["s"][h][:], 1.04, iou6[h][:], ALU.add, ALU.mult)
        for h in halves:
            nc.vector.tensor_reduce(zmax[h], z[h][:].rearrange("p (a v d) -> p a v d", a=2, d=D), AXIS_X, ALU.max)

        al = z
        almax = half_tiles("almax", GROUPS)
        for h in halves:
            nc.scalar.activation(almax[h][:].rearrange("p (a v) -> p a v", a=2), zmax[h], ACT.Sqrt, scale=0.5)
        for h in halves:
            nc.scalar.activation(al[h][:], z[h][:], ACT.Sqrt, scale=0.5 * 0.45 * 0.45)
        ls = [logs[:, 2 * h, :] for h in halves]
        lb = [logs[:, 2 * h + 1, :] for h in halves]
        for h in halves:
            nc.scalar.activation(ls[h], th["odds"][h][:], ACT.Ln, scale=25.49, bias=25.51)
        for h in halves:
            nc.scalar.activation(lb[h], th["s"][h][:], ACT.Ln, scale=-0.49, bias=0.51)

        mt = half_tiles("mt", GROUPS)
        inv = half_tiles("inv", GROUPS)
        ratio = half_tiles("ratio", GROUPS)
        nt = half_tiles("nt", COLS)
        gap = half_tiles("gap", COLS)
        gap2 = half_tiles("gap2", COLS)
        pos = half_tiles("pos", COLS)
        ce = half_tiles("ce", COLS)
        ql = half_tiles("ql", COLS)
        result = sb.tile([P, HALVES * GROUPS], F32, name="result")
        for h in halves:
            nc.vector.tensor_scalar(mt[h][:], almax[h][:], 0.01, None, ALU.add)
        for h in halves:
            nc.vector.reciprocal(inv[h][:], mt[h][:])
        for h in halves:
            nc.vector.scalar_tensor_tensor(ratio[h][:], mi[h][:], 0.5 / 0.45, inv[h][:], ALU.add, ALU.mult)
        for h in halves:
            nc.vector.tensor_tensor(grouped(nt[h][:]), grouped(al[h][:]), ratio[h][:].unsqueeze(2).to_broadcast([P, GROUPS, D]), ALU.mult)
        for h in halves:
            nc.vector.scalar_tensor_tensor(gap[h][:], th["s"][h][:], -0.5, nt[h][:], ALU.mult, ALU.add)
        for h in halves:
            nc.scalar.activation(gap2[h][:], gap[h][:], ACT.Square, bias=-0.5)
        for h in halves:
            nc.vector.tensor_tensor(pos[h][:], nt[h][:], ls[h], ALU.mult)
        for h in halves:
            nc.vector.tensor_tensor(ce[h][:], pos[h][:], lb[h], ALU.add)
        for h in halves:
            nc.vector.scalar_tensor_tensor(ql[h][:], ce[h][:], -1.0, gap2[h][:], ALU.mult, ALU.mult)
        for h in halves:
            nc.vector.tensor_reduce(result[:, h * GROUPS : (h + 1) * GROUPS], grouped(ql[h][:]), AXIS_X, ALU.add)
        nc.sync.dma_start(out, result[:])
